import numpy as np
import ml_dtypes


def mxq(x, axis, fmt="e4m3"):
    dtype, down = {"e4m3": (ml_dtypes.float8_e4m3fn, 7), "e5m2": (ml_dtypes.float8_e5m2, 14)}[fmt]
    v = np.moveaxis(np.asarray(x, np.float32).astype(ml_dtypes.bfloat16).astype(np.float64), axis, -1)
    blocks = v.reshape(v.shape[:-1] + (-1, 32))
    amax = np.abs(blocks).max(-1, keepdims=True)
    byte = np.maximum(np.where(amax > 0, np.frexp(amax)[1] - 1 + 127, 0) - down, 1)
    scale = np.exp2(byte - 127.0)
    codes = (blocks / scale).astype(np.float32).astype(dtype).astype(np.float64)
    return np.moveaxis((codes * scale).reshape(v.shape), -1, axis)


WIDE = False


def mx_kscale(k):
    if not WIDE:
        return np.ones(k)
    levels = np.array([10, -10, 5, -5, 0])
    if k % 512:
        return np.exp2(np.random.permutation(np.resize(levels, k // 32))).repeat(32)
    a = np.empty((k // 512, 16))
    for p in range(k // 512):
        a[p, :8] = np.random.permutation(np.resize(levels, 8))
        for g in range(8):
            far = levels[np.abs(levels - a[p, g]) >= 10]
            a[p, g + 8] = far[np.random.randint(len(far))]
    return np.exp2(a.ravel()).repeat(32)


def f64(x):
    return np.asarray(x).astype(np.float64)


def striped8(idx):
    return np.asarray(idx).reshape(8, -1, 16).transpose(0, 2, 1).reshape(128, -1).astype(np.uint16)


def unstriped8(offs):
    return offs.reshape(8, 16, -1).transpose(0, 2, 1).reshape(8, -1).astype(np.int64)


def pick8(x, idx, run):
    r = np.arange(len(x))
    return x[r[:, None], idx[r % (8 * run) // run]]


E2M1 = np.array([0.0, 0.5, 1.0, 1.5, 2.0, 3.0, 4.0, 6.0, -0.0, -0.5, -1.0, -1.5, -2.0, -3.0, -4.0, -6.0])


def pack_weight(w, fmt):
    k, n = w.shape
    w = f64(np.asarray(w, np.float32).astype(ml_dtypes.bfloat16)).reshape(k // 32, 32, n)
    amax = np.abs(w).max(1)
    if fmt == "e4m3":
        byte = np.frexp(amax)[1] - 1 + 127 - 7
    else:
        mant, ex = np.frexp(amax / 6.0)
        byte = np.where(mant > 0.5, ex, ex - 1) + 127
    byte = np.clip(np.where(amax > 0, byte, 1), 1, 254)
    scaled = (w * np.exp2(127.0 - byte)[:, None, :]).reshape(k, n).astype(np.float32)
    by_word = np.ascontiguousarray(scaled.reshape(k // 512, 128, 4, n).transpose(0, 1, 3, 2))
    if fmt == "e4m3":
        words = by_word.astype(ml_dtypes.float8_e4m3fn).view(np.uint8)
    else:
        c = by_word.astype(ml_dtypes.float4_e2m1fn).view(np.uint8) & 0xF
        words = (c[..., 0::2] | (c[..., 1::2] << 4)).reshape(k // 512, 128, 2 * n)
    return np.ascontiguousarray(words), np.ascontiguousarray(byte.astype(np.uint8).reshape(k // 512, 16, n))


def unpack_weight(words, scales, fmt):
    g, _, n = scales.shape
    words = np.ascontiguousarray(words).reshape(g, 128, n, -1)
    if fmt == "e4m3":
        vals = words.view(ml_dtypes.float8_e4m3fn).astype(np.float64)
    else:
        nib = np.empty((g, 128, n, 4), np.uint8)
        nib[..., 0::2] = words & 0xF
        nib[..., 1::2] = words >> 4
        vals = E2M1[nib]
    vals = vals * np.repeat(np.exp2(scales.astype(np.float64) - 127.0), 8, axis=1)[..., None]
    return vals.transpose(0, 1, 3, 2).reshape(g * 512, n)


D, T, I, Q = 512, 1024, 512, 128


def setup_inputs():
    n = np.random.standard_normal
    idx = np.stack([np.random.permutation(T)[:I] for _ in range(8)])
    idx2 = np.stack([np.random.permutation(T)[:I] for _ in range(8)])
    idx3 = np.stack([np.random.permutation(T)[:I] for _ in range(8)])
    idx4 = np.stack([np.random.permutation(T)[:I] for _ in range(8)])
    fd = mx_kscale(D)
    keysp = pack_weight(n((D, T)) / fd[:, None], "e4m3")
    return {
        "query": (n((D, Q)) * 0.9 / np.sqrt(D) * fd[:, None]).astype(np.float32),
        "keys_words": keysp[0],
        "keys_scales": keysp[1],
        "lam": (np.random.uniform(0.3, 0.9, (Q, 1))).astype(np.float32),
        "reserve": (np.random.uniform(0.5, 2.0, (Q, 1))).astype(np.float32),
        "old": (np.random.uniform(0.0, 2.0, (Q, T))).astype(np.float32),
        "gainm": (np.random.uniform(0.5, 1.5, (Q, I))).astype(np.float32),
        "offs": striped8(idx),
        "offs2": striped8(idx2),
        "offs3": striped8(idx3),
        "offs4": striped8(idx4),
    }


def reference(query, keys_words, keys_scales, lam, reserve, old, gainm, offs, offs2, offs3, offs4):
    idx = unstriped8(offs)
    idx2 = unstriped8(offs2)
    idx3 = unstriped8(offs3)
    idx4 = unstriped8(offs4)
    keysu = unpack_weight(keys_words, keys_scales, "e4m3")
    queryq = mxq(f64(query), 0, "e4m3")
    a = queryq.T @ keysu
    s = pick8(a, idx, 16) + np.maximum(pick8(a, idx2, 16), pick8(a, idx3, 16)) * f64(lam)
    p = np.exp(s - np.max(s, axis=1, keepdims=True))
    r = p / np.sum(p, axis=1, keepdims=True)
    u0 = r * np.log(r) * (-1.0)
    w = u0 / (np.sum(u0, axis=1, keepdims=True) + f64(reserve))
    ws = w * f64(gainm) * 512.0
    wf = np.zeros((Q, T))
    wf[np.arange(Q)[:, None], idx4[np.arange(Q) % 128 // 16]] = ws
    y = f64(old) + wf
    return y

@@ -1,0 +1,191 @@
+import math
+from contextlib import ExitStack
+
+import concourse.mybir as mybir
+
+D, T, SLOTS, Q = 512, 1024, 512, 128
+FLOPS = 2 * D * Q * T
+
+F32 = mybir.dt.float32
+BF16 = mybir.dt.bfloat16
+I32 = mybir.dt.int32
+U32 = mybir.dt.uint32
+U16 = mybir.dt.uint16
+U8 = mybir.dt.uint8
+FP8X4 = mybir.dt.float8_e4m3fn_x4
+ALU = mybir.AluOpType
+ACT = mybir.ActivationFunctionType
+
+P = 128
+PACK = 4
+KEY_LOAD = 512
+PASS_N = 256
+HALF = SLOTS // 2
+LIST_COLS = HALF // 16
+OUT_CHUNK = 256
+
+LN_PER_BIT = math.log(2.0) / 2.0**23
+LN_OFFSET = 88.0
+SERIES = 16
+
+
+def tile_attend_lookahead_lacking_moved_heads_kernel(
+    tc, query, keys_words, keys_scales, lam, reserve, old, gainm, offs, offs2, offs3, offs4, out
+):
+    nc = tc.nc
+    with ExitStack() as ctx:
+        pool = ctx.enter_context(tc.tile_pool(name="pool", bufs=1))
+        psum = ctx.enter_context(tc.psum_pool(name="psum", bufs=1))
+
+        k_scales = pool.tile([P, T], U8, align_bytes=64)
+        nc.vector.memset(k_scales[:].bitcast(I32), 0)
+
+        q_raw = pool.tile([P, PACK, Q], F32)
+        nc.sync.dma_start(out=q_raw[:], in_=query.rearrange("(p j) q -> p j q", j=PACK))
+        for quad in range(4):
+            nc.sync.dma_start(
+                out=k_scales[32 * quad : 32 * quad + 4, :].bitcast(I32),
+                in_=keys_scales[0, 4 * quad : 4 * quad + 4, :].bitcast(I32),
+            )
+        words_hbm = keys_words[0].rearrange("p n t -> p (n t)").bitcast(I32)
+        k_words = []
+        for c0 in range(0, T, KEY_LOAD):
+            words = pool.tile([P, KEY_LOAD], I32, align_bytes=64, name=f"k_words{c0}")
+            nc.sync.dma_start(out=words[:], in_=words_hbm[:, c0 : c0 + KEY_LOAD])
+            k_words.append(words)
+
+        def load(src, shape, dtype, name):
+            tile = pool.tile(shape, dtype, name=name)
+            nc.sync.dma_start(out=tile[:], in_=src)
+            return tile
+
+        list2 = load(offs2, [P, SLOTS // 16], U16, "list2")
+        list3 = load(offs3, [P, SLOTS // 16], U16, "list3")
+        list1 = load(offs, [P, SLOTS // 16], U16, "list1")
+        lam_sb = load(lam, [P, 1], F32, "lam_sb")
+        reserve_sb = load(reserve, [P, 1], F32, "reserve_sb")
+        gain_sb = load(gainm, [P, SLOTS], F32, "gain_sb")
+        list4 = load(offs4, [P, SLOTS // 16], U16, "list4")
+        old_sb = load(old, [P, T], F32, "old_sb")
+
+        steps = SERIES + 4
+        c_log, c_res, c_den, c_out = SERIES, SERIES + 1, SERIES + 2, SERIES + 3
+        factor = pool.tile([P, steps], F32)
+        addend = pool.tile([P, steps], F32)
+        orders = pool.tile([P, SERIES], F32)
+        for first, base, step in ((0, -SERIES, 2), (1, SERIES - 1, -2)):
+            nc.gpsimd.iota(
+                orders[:, first:SERIES:2],
+                [[step, SERIES // 2]],
+                base=base,
+                channel_multiplier=0,
+                allow_small_or_imprecise_dtypes=True,
+            )
+        nc.vector.memset(factor[:, c_res : c_res + 1], 1.0)
+        nc.scalar.activation(
+            factor[:, c_out : c_out + 1], factor[:, c_res : c_res + 1], ACT.Copy, scale=1.0 / 512.0
+        )
+        nc.vector.memset(addend[:, c_out : c_out + 1], 0.0)
+        nc.vector.reciprocal(addend[:, 0:SERIES], orders[:])
+        placed = pool.tile([P, T], F32)
+        nc.vector.memset(placed[:], 0.0)
+
+        q_grouped = pool.tile([P, Q, PACK], BF16, align_bytes=64)
+        nc.vector.tensor_copy(
+            out=q_grouped[:].rearrange("p (c i) j -> p c j i", i=4),
+            in_=q_raw[:].rearrange("p j (c i) -> p c j i", i=4),
+        )
+        q_words = pool.tile([P, Q], U32, align_bytes=64)
+        q_scales = pool.tile([P, Q], U8, align_bytes=64)
+        nc.vector.quantize_mx(
+            out=q_words[:].bitcast(FP8X4),
+            scales=q_scales[:],
+            in_=q_grouped[:].rearrange("p q j -> p (q j)"),
+        )
+
+        scores = pool.tile([P, T], F32)
+        for n, c0 in enumerate(range(0, T, PASS_N)):
+            acc = psum.tile([Q, PASS_N], F32, name=f"acc{n}")
+            w0 = c0 % KEY_LOAD
+            nc.tensor.matmul_mx(
+                out=acc[:],
+                lhsT=q_words[:].bitcast(FP8X4),
+                lhsT_scale=q_scales[:],
+                rhs=k_words[c0 // KEY_LOAD][:, w0 : w0 + PASS_N].bitcast(FP8X4),
+                rhs_scale=k_scales[:, c0 : c0 + PASS_N],
+                start=True,
+                stop=True,
+            )
+            if n % 2 == 0:
+                nc.scalar.copy(out=scores[:, c0 : c0 + PASS_N], in_=acc[:])
+            else:
+                nc.vector.tensor_copy(out=scores[:, c0 : c0 + PASS_N], in_=acc[:])
+
+        own = pool.tile([P, HALF], F32)
+        fol2 = pool.tile([P, SLOTS], F32)
+        fol3 = pool.tile([P, SLOTS], F32)
+        best = pool.tile([P, SLOTS], F32)
+        ahead = pool.tile([P, HALF], F32)
+        s = pool.tile([P, SLOTS], F32)
+        neg_s = pool.tile([P, SLOTS], F32)
+        neg_max = pool.tile([P, 2], F32)
+
+        def window(lists, h):
+            return scores[:].indirect(lists[:, h * LIST_COLS : (h + 1) * LIST_COLS])
+
+        lo, hi = slice(0, HALF), slice(HALF, SLOTS)
+        nc.scalar.activation(fol2[:, lo], window(list2, 0), ACT.Copy)
+        nc.scalar.activation(fol2[:, hi], window(list2, 1), ACT.Copy)
+        nc.scalar.activation(own[:], window(list1, 1), ACT.Copy)
+        nc.vector.tensor_copy(fol3[:, lo], window(list3, 0))
+        nc.vector.tensor_copy(fol3[:, hi], window(list3, 1))
+        nc.vector.tensor_tensor(best[:, lo], fol2[:, lo], fol3[:, lo], ALU.max)
+        nc.vector.tensor_tensor(best[:, hi], fol2[:, hi], fol3[:, hi], ALU.max)
+        nc.vector.tensor_scalar(ahead[:], best[:, lo], lam_sb[:], None, ALU.mult)
+        nc.vector.tensor_tensor(s[:, lo], window(list1, 0), ahead[:], ALU.add)
+        nc.vector.scalar_tensor_tensor(s[:, hi], best[:, hi], lam_sb[:], own[:], ALU.mult, ALU.add)
+        nc.vector.tensor_scalar(
+            neg_s[:, lo], s[:, lo], -1.0, None, ALU.mult, ALU.min, accum_out=neg_max[:, 0:1]
+        )
+        nc.vector.tensor_scalar(
+            neg_s[:, hi], s[:, hi], -1.0, neg_max[:, 0:1], ALU.mult, ALU.min, accum_out=neg_max[:, 1:2]
+        )
+        neg_m = neg_max[:, 1:2]
+
+        p = pool.tile([P, SLOTS], F32)
+        z = factor[:, c_den : c_den + 1]
+        nc.scalar.activation(p[:], s[:], ACT.Exp, bias=neg_m, accum_out=z)
+        guess_bias = pool.tile([P, 1], F32)
+        nc.vector.tensor_scalar(guess_bias[:], neg_m, -1.0, -LN_OFFSET, ALU.mult, ALU.add)
+        nc.vector.tensor_tensor(addend[:, c_res : c_res + 1], reserve_sb[:], neg_m, ALU.add)
+
+        inv_guess = pool.tile([P, 1], F32)
+        nc.scalar.activation(inv_guess[:], z.bitcast(U32), ACT.Exp, scale=-LN_PER_BIT, bias=LN_OFFSET)
+        nc.scalar.activation(
+            addend[:, c_log : c_log + 1], z.bitcast(U32), ACT.Identity, scale=LN_PER_BIT, bias=guess_bias[:]
+        )
+        nc.scalar.activation(
+            factor[:, 0 : c_log + 1], inv_guess[:].to_broadcast([P, c_log + 1]), ACT.Identity, scale=z, bias=-1.0
+        )
+
+        gap_p = pool.tile([P, SLOTS], F32)
+        nc.vector.scalar_tensor_tensor(
+            gap_p[:], neg_s[:], neg_m, p[:], ALU.subtract, ALU.mult, accum_out=addend[:, c_den : c_den + 1]
+        )
+        scan = pool.tile([P, steps], F32)
+        nc.vector.tensor_tensor_scan(scan[:], factor[:], addend[:], 0.0, ALU.mult, ALU.add)
+        row_scale = pool.tile([P, 1], F32)
+        nc.vector.reciprocal(row_scale[:], scan[:, c_out : c_out + 1])
+        neg_log = pool.tile([P, SLOTS], F32)
+        nc.scalar.activation(neg_log[:], neg_s[:], ACT.Identity, bias=scan[:, c_log : c_log + 1])
+        scaled = pool.tile([P, SLOTS], F32)
+        nc.vector.scalar_tensor_tensor(scaled[:], p[:], row_scale[:], gain_sb[:], ALU.mult, ALU.mult)
+
+        nc.vector.tensor_tensor(placed[:].indirect(list4[:]), scaled[:], neg_log[:], ALU.mult)
+
+        for n, c0 in enumerate(range(0, T, OUT_CHUNK)):
+            cols = slice(c0, c0 + OUT_CHUNK)
+            total = pool.tile([P, OUT_CHUNK], F32, name=f"total{n}")
+            nc.vector.tensor_tensor(total[:], placed[:, cols], old_sb[:, cols], ALU.add)
+            queue = nc.sync if n % 2 == 0 else nc.scalar
+            queue.dma_start(out=out[:, cols], in_=total[:])

@@ -19,7 +19,7 @@ ACT = mybir.ActivationFunctionType
 P = 128
 PACK = 4
 KEY_LOAD = 512
-PASS_N = 256
+PASS_WIDTHS = (256, 256, 256, 128, 128)
 HALF = SLOTS // 2
 LIST_COLS = HALF // 16
 OUT_CHUNK = 256
@@ -42,17 +42,17 @@ def tile_attend_lookahead_lacking_moved_heads_kernel(
 
         q_raw = pool.tile([P, PACK, Q], F32)
         nc.sync.dma_start(out=q_raw[:], in_=query.rearrange("(p j) q -> p j q", j=PACK))
+        words_hbm = keys_words[0].rearrange("p n t -> p (n t)").bitcast(I32)
+        k_words = [
+            pool.tile([P, KEY_LOAD], I32, align_bytes=64, name=f"k_words{n}") for n in range(T // KEY_LOAD)
+        ]
+        nc.sync.dma_start(out=k_words[0][:], in_=words_hbm[:, 0:KEY_LOAD])
         for quad in range(4):
             nc.sync.dma_start(
                 out=k_scales[32 * quad : 32 * quad + 4, :].bitcast(I32),
                 in_=keys_scales[0, 4 * quad : 4 * quad + 4, :].bitcast(I32),
             )
-        words_hbm = keys_words[0].rearrange("p n t -> p (n t)").bitcast(I32)
-        k_words = []
-        for c0 in range(0, T, KEY_LOAD):
-            words = pool.tile([P, KEY_LOAD], I32, align_bytes=64, name=f"k_words{c0}")
-            nc.sync.dma_start(out=words[:], in_=words_hbm[:, c0 : c0 + KEY_LOAD])
-            k_words.append(words)
+        nc.sync.dma_start(out=k_words[1][:], in_=words_hbm[:, KEY_LOAD:T])
 
         def load(src, shape, dtype, name):
             tile = pool.tile(shape, dtype, name=name)
@@ -68,10 +68,11 @@ def tile_attend_lookahead_lacking_moved_heads_kernel(
         list4 = load(offs4, [P, SLOTS // 16], U16, "list4")
         old_sb = load(old, [P, T], F32, "old_sb")
 
-        steps = SERIES + 4
-        c_log, c_res, c_den, c_out = SERIES, SERIES + 1, SERIES + 2, SERIES + 3
-        factor = pool.tile([P, steps], F32)
-        addend = pool.tile([P, steps], F32)
+        steps = SERIES + 5
+        c_log, c_res, c_den, c_one, c_out = range(SERIES, steps)
+        p_gain = pool.tile([P, SLOTS], F32)
+        factor = p_gain[:, HALF : HALF + steps]
+        addend = p_gain[:, SLOTS - steps : SLOTS]
         orders = pool.tile([P, SERIES], F32)
         for first, base, step in ((0, -SERIES, 2), (1, SERIES - 1, -2)):
             nc.gpsimd.iota(
@@ -82,6 +83,7 @@ def tile_attend_lookahead_lacking_moved_heads_kernel(
                 allow_small_or_imprecise_dtypes=True,
             )
         nc.vector.memset(factor[:, c_res : c_res + 1], 1.0)
+        nc.vector.memset(factor[:, c_one : c_one + 1], 1.0)
         nc.scalar.activation(
             factor[:, c_out : c_out + 1], factor[:, c_res : c_res + 1], ACT.Copy, scale=1.0 / 512.0
         )
@@ -104,28 +106,29 @@ def tile_attend_lookahead_lacking_moved_heads_kernel(
         )
 
         scores = pool.tile([P, T], F32)
-        for n, c0 in enumerate(range(0, T, PASS_N)):
-            acc = psum.tile([Q, PASS_N], F32, name=f"acc{n}")
+        c0 = 0
+        for n, width in enumerate(PASS_WIDTHS):
+            acc = psum.tile([Q, width], F32, name=f"acc{n}")
             w0 = c0 % KEY_LOAD
             nc.tensor.matmul_mx(
                 out=acc[:],
                 lhsT=q_words[:].bitcast(FP8X4),
                 lhsT_scale=q_scales[:],
-                rhs=k_words[c0 // KEY_LOAD][:, w0 : w0 + PASS_N].bitcast(FP8X4),
-                rhs_scale=k_scales[:, c0 : c0 + PASS_N],
+                rhs=k_words[c0 // KEY_LOAD][:, w0 : w0 + width].bitcast(FP8X4),
+                rhs_scale=k_scales[:, c0 : c0 + width],
                 start=True,
                 stop=True,
             )
             if n % 2 == 0:
-                nc.scalar.copy(out=scores[:, c0 : c0 + PASS_N], in_=acc[:])
+                nc.scalar.copy(out=scores[:, c0 : c0 + width], in_=acc[:])
             else:
-                nc.vector.tensor_copy(out=scores[:, c0 : c0 + PASS_N], in_=acc[:])
+                nc.vector.tensor_copy(out=scores[:, c0 : c0 + width], in_=acc[:])
+            c0 = c0 + width
 
-        own = pool.tile([P, HALF], F32)
+        own = pool.tile([P, SLOTS], F32)
         fol2 = pool.tile([P, SLOTS], F32)
         fol3 = pool.tile([P, SLOTS], F32)
         best = pool.tile([P, SLOTS], F32)
-        ahead = pool.tile([P, HALF], F32)
         s = pool.tile([P, SLOTS], F32)
         neg_s = pool.tile([P, SLOTS], F32)
         neg_max = pool.tile([P, 2], F32)
@@ -134,30 +137,53 @@ def tile_attend_lookahead_lacking_moved_heads_kernel(
             return scores[:].indirect(lists[:, h * LIST_COLS : (h + 1) * LIST_COLS])
 
         lo, hi = slice(0, HALF), slice(HALF, SLOTS)
-        nc.scalar.activation(fol2[:, lo], window(list2, 0), ACT.Copy)
-        nc.scalar.activation(fol2[:, hi], window(list2, 1), ACT.Copy)
-        nc.scalar.activation(own[:], window(list1, 1), ACT.Copy)
-        nc.vector.tensor_copy(fol3[:, lo], window(list3, 0))
-        nc.vector.tensor_copy(fol3[:, hi], window(list3, 1))
-        nc.vector.tensor_tensor(best[:, lo], fol2[:, lo], fol3[:, lo], ALU.max)
-        nc.vector.tensor_tensor(best[:, hi], fol2[:, hi], fol3[:, hi], ALU.max)
-        nc.vector.tensor_scalar(ahead[:], best[:, lo], lam_sb[:], None, ALU.mult)
-        nc.vector.tensor_tensor(s[:, lo], window(list1, 0), ahead[:], ALU.add)
-        nc.vector.scalar_tensor_tensor(s[:, hi], best[:, hi], lam_sb[:], own[:], ALU.mult, ALU.add)
-        nc.vector.tensor_scalar(
-            neg_s[:, lo], s[:, lo], -1.0, None, ALU.mult, ALU.min, accum_out=neg_max[:, 0:1]
-        )
-        nc.vector.tensor_scalar(
-            neg_s[:, hi], s[:, hi], -1.0, neg_max[:, 0:1], ALU.mult, ALU.min, accum_out=neg_max[:, 1:2]
-        )
-        neg_m = neg_max[:, 1:2]
+        halves = (lo, hi)
+        for h, cols in enumerate(halves):
+            nc.scalar.activation(fol2[:, cols], window(list2, h), ACT.Copy)
+            nc.vector.tensor_copy(fol3[:, cols], window(list3, h))
+        for h, cols in enumerate(halves):
+            nc.scalar.activation(own[:, cols], window(list1, h), ACT.Copy)
+            nc.vector.tensor_tensor(best[:, cols], fol2[:, cols], fol3[:, cols], ALU.max)
+        for h, cols in enumerate(halves):
+            nc.vector.scalar_tensor_tensor(s[:, cols], best[:, cols], lam_sb[:], own[:, cols], ALU.mult, ALU.add)
+            nc.vector.tensor_scalar(
+                neg_s[:, cols],
+                s[:, cols],
+                -1.0,
+                neg_max[:, 0:1] if h else None,
+                ALU.mult,
+                ALU.min,
+                accum_out=neg_max[:, h : h + 1],
+            )
+        neg_m_lo, neg_m = neg_max[:, 0:1], neg_max[:, 1:2]
 
         p = pool.tile([P, SLOTS], F32)
+        sums = pool.tile([P, 3], F32)
+        z_lo, z_hi, gap_lo = sums[:, 0:1], sums[:, 1:2], sums[:, 2:3]
+        rescale = pool.tile([P, 1], F32)
         z = factor[:, c_den : c_den + 1]
-        nc.scalar.activation(p[:], s[:], ACT.Exp, bias=neg_m, accum_out=z)
+        nc.scalar.activation(p[:, lo], s[:, lo], ACT.Exp, bias=neg_m_lo, accum_out=z_lo)
+        nc.scalar.activation(rescale[:], neg_m_lo, ACT.Exp, scale=-1.0, bias=neg_m)
+        nc.scalar.activation(p[:, hi], s[:, hi], ACT.Exp, bias=neg_m, accum_out=z_hi)
+        nc.scalar.activation(z, z_lo, ACT.Identity, scale=rescale[:], bias=z_hi)
+
+        gap_p = pool.tile([P, SLOTS], F32)
+        nc.vector.scalar_tensor_tensor(
+            gap_p[:, lo], neg_s[:, lo], neg_m, p[:, lo], ALU.subtract, ALU.mult, accum_out=gap_lo
+        )
         guess_bias = pool.tile([P, 1], F32)
         nc.vector.tensor_scalar(guess_bias[:], neg_m, -1.0, -LN_OFFSET, ALU.mult, ALU.add)
         nc.vector.tensor_tensor(addend[:, c_res : c_res + 1], reserve_sb[:], neg_m, ALU.add)
+        nc.vector.scalar_tensor_tensor(p_gain[:, lo], p[:, lo], rescale[:], gain_sb[:, lo], ALU.mult, ALU.mult)
+        nc.vector.scalar_tensor_tensor(
+            gap_p[:, hi],
+            neg_s[:, hi],
+            neg_m,
+            p[:, hi],
+            ALU.subtract,
+            ALU.mult,
+            accum_out=addend[:, c_den : c_den + 1],
+        )
 
         inv_guess = pool.tile([P, 1], F32)
         nc.scalar.activation(inv_guess[:], z.bitcast(U32), ACT.Exp, scale=-LN_PER_BIT, bias=LN_OFFSET)
@@ -167,21 +193,19 @@ def tile_attend_lookahead_lacking_moved_heads_kernel(
         nc.scalar.activation(
             factor[:, 0 : c_log + 1], inv_guess[:].to_broadcast([P, c_log + 1]), ACT.Identity, scale=z, bias=-1.0
         )
+        nc.scalar.activation(addend[:, c_one : c_one + 1], gap_lo, ACT.Copy, scale=rescale[:])
 
-        gap_p = pool.tile([P, SLOTS], F32)
-        nc.vector.scalar_tensor_tensor(
-            gap_p[:], neg_s[:], neg_m, p[:], ALU.subtract, ALU.mult, accum_out=addend[:, c_den : c_den + 1]
-        )
         scan = pool.tile([P, steps], F32)
-        nc.vector.tensor_tensor_scan(scan[:], factor[:], addend[:], 0.0, ALU.mult, ALU.add)
+        nc.vector.tensor_tensor_scan(scan[:], factor, addend, 0.0, ALU.mult, ALU.add)
+        nc.vector.tensor_tensor(p_gain[:, hi], p[:, hi], gain_sb[:, hi], ALU.mult)
         row_scale = pool.tile([P, 1], F32)
         nc.vector.reciprocal(row_scale[:], scan[:, c_out : c_out + 1])
         neg_log = pool.tile([P, SLOTS], F32)
-        nc.scalar.activation(neg_log[:], neg_s[:], ACT.Identity, bias=scan[:, c_log : c_log + 1])
-        scaled = pool.tile([P, SLOTS], F32)
-        nc.vector.scalar_tensor_tensor(scaled[:], p[:], row_scale[:], gain_sb[:], ALU.mult, ALU.mult)
+        nc.vector.tensor_scalar(
+            neg_log[:], neg_s[:], scan[:, c_log : c_log + 1], row_scale[:], ALU.add, ALU.mult
+        )
 
-        nc.vector.tensor_tensor(placed[:].indirect(list4[:]), scaled[:], neg_log[:], ALU.mult)
+        nc.vector.tensor_tensor(placed[:].indirect(list4[:]), p_gain[:], neg_log[:], ALU.mult)
 
         for n, c0 in enumerate(range(0, T, OUT_CHUNK)):
             cols = slice(c0, c0 + OUT_CHUNK)

@@ -22,7 +22,7 @@ KEY_LOAD = 512
 PASS_WIDTHS = (256, 256, 256, 128, 128)
 HALF = SLOTS // 2
 LIST_COLS = HALF // 16
-OUT_CHUNK = 256
+OUT_WIDTHS = (128, 256, 256, 256, 128)
 
 LN_PER_BIT = math.log(2.0) / 2.0**23
 LN_OFFSET = 88.0
@@ -93,10 +93,11 @@ def tile_attend_lookahead_lacking_moved_heads_kernel(
         nc.vector.memset(placed[:], 0.0)
 
         q_grouped = pool.tile([P, Q, PACK], BF16, align_bytes=64)
-        nc.vector.tensor_copy(
-            out=q_grouped[:].rearrange("p (c i) j -> p c j i", i=4),
-            in_=q_raw[:].rearrange("p j (c i) -> p c j i", i=4),
-        )
+        for copy, rows in ((nc.vector.tensor_copy, slice(0, Q // 2)), (nc.scalar.copy, slice(Q // 2, Q))):
+            copy(
+                out=q_grouped[:, rows, :].rearrange("p (c i) j -> p c j i", i=4),
+                in_=q_raw[:, :, rows].rearrange("p j (c i) -> p c j i", i=4),
+            )
         q_words = pool.tile([P, Q], U32, align_bytes=64)
         q_scales = pool.tile([P, Q], U8, align_bytes=64)
         nc.vector.quantize_mx(
@@ -197,9 +198,9 @@ def tile_attend_lookahead_lacking_moved_heads_kernel(
 
         scan = pool.tile([P, steps], F32)
         nc.vector.tensor_tensor_scan(scan[:], factor, addend, 0.0, ALU.mult, ALU.add)
-        nc.vector.tensor_tensor(p_gain[:, hi], p[:, hi], gain_sb[:, hi], ALU.mult)
         row_scale = pool.tile([P, 1], F32)
         nc.vector.reciprocal(row_scale[:], scan[:, c_out : c_out + 1])
+        nc.vector.tensor_tensor(p_gain[:, hi], p[:, hi], gain_sb[:, hi], ALU.mult)
         neg_log = pool.tile([P, SLOTS], F32)
         nc.vector.tensor_scalar(
             neg_log[:], neg_s[:], scan[:, c_log : c_log + 1], row_scale[:], ALU.add, ALU.mult
@@ -207,9 +208,11 @@ def tile_attend_lookahead_lacking_moved_heads_kernel(
 
         nc.vector.tensor_tensor(placed[:].indirect(list4[:]), p_gain[:], neg_log[:], ALU.mult)
 
-        for n, c0 in enumerate(range(0, T, OUT_CHUNK)):
-            cols = slice(c0, c0 + OUT_CHUNK)
-            total = pool.tile([P, OUT_CHUNK], F32, name=f"total{n}")
+        c0 = 0
+        for n, width in enumerate(OUT_WIDTHS):
+            cols = slice(c0, c0 + width)
+            total = pool.tile([P, width], F32, name=f"total{n}")
             nc.vector.tensor_tensor(total[:], placed[:, cols], old_sb[:, cols], ALU.add)
             queue = nc.sync if n % 2 == 0 else nc.scalar
             queue.dma_start(out=out[:, cols], in_=total[:])
+            c0 = c0 + width

import math
from contextlib import ExitStack

import concourse.mybir as mybir

D, T, SLOTS, Q = 512, 1024, 512, 128
FLOPS = 2 * D * Q * T

F32 = mybir.dt.float32
BF16 = mybir.dt.bfloat16
I32 = mybir.dt.int32
U32 = mybir.dt.uint32
U16 = mybir.dt.uint16
U8 = mybir.dt.uint8
FP8X4 = mybir.dt.float8_e4m3fn_x4
ALU = mybir.AluOpType
ACT = mybir.ActivationFunctionType

P = 128
PACK = 4
KEY_LOAD = 512
PASS_WIDTHS = (256, 256, 256, 128, 128)
HALF = SLOTS // 2
LIST_COLS = HALF // 16
OUT_WIDTHS = (128, 256, 256, 256, 128)

LN_PER_BIT = math.log(2.0) / 2.0**23
LN_OFFSET = 88.0
SERIES = 16


def tile_attend_lookahead_lacking_moved_heads_kernel(
    tc, query, keys_words, keys_scales, lam, reserve, old, gainm, offs, offs2, offs3, offs4, out
):
    nc = tc.nc
    with ExitStack() as ctx:
        pool = ctx.enter_context(tc.tile_pool(name="pool", bufs=1))
        psum = ctx.enter_context(tc.psum_pool(name="psum", bufs=1))

        k_scales = pool.tile([P, T], U8, align_bytes=64)
        nc.vector.memset(k_scales[:].bitcast(I32), 0)

        q_raw = pool.tile([P, PACK, Q], F32)
        nc.sync.dma_start(out=q_raw[:], in_=query.rearrange("(p j) q -> p j q", j=PACK))
        words_hbm = keys_words[0].rearrange("p n t -> p (n t)").bitcast(I32)
        k_words = [
            pool.tile([P, KEY_LOAD], I32, align_bytes=64, name=f"k_words{n}") for n in range(T // KEY_LOAD)
        ]
        nc.sync.dma_start(out=k_words[0][:], in_=words_hbm[:, 0:KEY_LOAD])
        for quad in range(4):
            nc.sync.dma_start(
                out=k_scales[32 * quad : 32 * quad + 4, :].bitcast(I32),
                in_=keys_scales[0, 4 * quad : 4 * quad + 4, :].bitcast(I32),
            )
        nc.sync.dma_start(out=k_words[1][:], in_=words_hbm[:, KEY_LOAD:T])

        def load(src, shape, dtype, name):
            tile = pool.tile(shape, dtype, name=name)
            nc.sync.dma_start(out=tile[:], in_=src)
            return tile

        list2 = load(offs2, [P, SLOTS // 16], U16, "list2")
        list3 = load(offs3, [P, SLOTS // 16], U16, "list3")
        list1 = load(offs, [P, SLOTS // 16], U16, "list1")
        lam_sb = load(lam, [P, 1], F32, "lam_sb")
        reserve_sb = load(reserve, [P, 1], F32, "reserve_sb")
        gain_sb = load(gainm, [P, SLOTS], F32, "gain_sb")
        list4 = load(offs4, [P, SLOTS // 16], U16, "list4")
        old_sb = load(old, [P, T], F32, "old_sb")

        steps = SERIES + 5
        c_log, c_res, c_den, c_one, c_out = range(SERIES, steps)
        p_gain = pool.tile([P, SLOTS], F32)
        factor = p_gain[:, HALF : HALF + steps]
        addend = p_gain[:, SLOTS - steps : SLOTS]
        orders = pool.tile([P, SERIES], F32)
        for first, base, step in ((0, -SERIES, 2), (1, SERIES - 1, -2)):
            nc.gpsimd.iota(
                orders[:, first:SERIES:2],
                [[step, SERIES // 2]],
                base=base,
                channel_multiplier=0,
                allow_small_or_imprecise_dtypes=True,
            )
        nc.vector.memset(factor[:, c_res : c_res + 1], 1.0)
        nc.vector.memset(factor[:, c_one : c_one + 1], 1.0)
        nc.scalar.activation(
            factor[:, c_out : c_out + 1], factor[:, c_res : c_res + 1], ACT.Copy, scale=1.0 / 512.0
        )
        nc.vector.memset(addend[:, c_out : c_out + 1], 0.0)
        nc.vector.reciprocal(addend[:, 0:SERIES], orders[:])
        placed = pool.tile([P, T], F32)
        nc.vector.memset(placed[:], 0.0)

        q_grouped = pool.tile([P, Q, PACK], BF16, align_bytes=64)
        for copy, rows in ((nc.vector.tensor_copy, slice(0, Q // 2)), (nc.scalar.copy, slice(Q // 2, Q))):
            copy(
                out=q_grouped[:, rows, :].rearrange("p (c i) j -> p c j i", i=4),
                in_=q_raw[:, :, rows].rearrange("p j (c i) -> p c j i", i=4),
            )
        q_words = pool.tile([P, Q], U32, align_bytes=64)
        q_scales = pool.tile([P, Q], U8, align_bytes=64)
        nc.vector.quantize_mx(
            out=q_words[:].bitcast(FP8X4),
            scales=q_scales[:],
            in_=q_grouped[:].rearrange("p q j -> p (q j)"),
        )

        scores = pool.tile([P, T], F32)
        c0 = 0
        for n, width in enumerate(PASS_WIDTHS):
            acc = psum.tile([Q, width], F32, name=f"acc{n}")
            w0 = c0 % KEY_LOAD
            nc.tensor.matmul_mx(
                out=acc[:],
                lhsT=q_words[:].bitcast(FP8X4),
                lhsT_scale=q_scales[:],
                rhs=k_words[c0 // KEY_LOAD][:, w0 : w0 + width].bitcast(FP8X4),
                rhs_scale=k_scales[:, c0 : c0 + width],
                start=True,
                stop=True,
            )
            if n % 2 == 0:
                nc.scalar.copy(out=scores[:, c0 : c0 + width], in_=acc[:])
            else:
                nc.vector.tensor_copy(out=scores[:, c0 : c0 + width], in_=acc[:])
            c0 = c0 + width

        own = pool.tile([P, SLOTS], F32)
        fol2 = pool.tile([P, SLOTS], F32)
        fol3 = pool.tile([P, SLOTS], F32)
        best = pool.tile([P, SLOTS], F32)
        s = pool.tile([P, SLOTS], F32)
        neg_s = pool.tile([P, SLOTS], F32)
        neg_max = pool.tile([P, 2], F32)

        def window(lists, h):
            return scores[:].indirect(lists[:, h * LIST_COLS : (h + 1) * LIST_COLS])

        lo, hi = slice(0, HALF), slice(HALF, SLOTS)
        halves = (lo, hi)
        for h, cols in enumerate(halves):
            nc.scalar.activation(fol2[:, cols], window(list2, h), ACT.Copy)
            nc.vector.tensor_copy(fol3[:, cols], window(list3, h))
        for h, cols in enumerate(halves):
            nc.scalar.activation(own[:, cols], window(list1, h), ACT.Copy)
            nc.vector.tensor_tensor(best[:, cols], fol2[:, cols], fol3[:, cols], ALU.max)
        for h, cols in enumerate(halves):
            nc.vector.scalar_tensor_tensor(s[:, cols], best[:, cols], lam_sb[:], own[:, cols], ALU.mult, ALU.add)
            nc.vector.tensor_scalar(
                neg_s[:, cols],
                s[:, cols],
                -1.0,
                neg_max[:, 0:1] if h else None,
                ALU.mult,
                ALU.min,
                accum_out=neg_max[:, h : h + 1],
            )
        neg_m_lo, neg_m = neg_max[:, 0:1], neg_max[:, 1:2]

        p = pool.tile([P, SLOTS], F32)
        sums = pool.tile([P, 3], F32)
        z_lo, z_hi, gap_lo = sums[:, 0:1], sums[:, 1:2], sums[:, 2:3]
        rescale = pool.tile([P, 1], F32)
        z = factor[:, c_den : c_den + 1]
        nc.scalar.activation(p[:, lo], s[:, lo], ACT.Exp, bias=neg_m_lo, accum_out=z_lo)
        nc.scalar.activation(rescale[:], neg_m_lo, ACT.Exp, scale=-1.0, bias=neg_m)
        nc.scalar.activation(p[:, hi], s[:, hi], ACT.Exp, bias=neg_m, accum_out=z_hi)
        nc.scalar.activation(z, z_lo, ACT.Identity, scale=rescale[:], bias=z_hi)

        gap_p = pool.tile([P, SLOTS], F32)
        nc.vector.scalar_tensor_tensor(
            gap_p[:, lo], neg_s[:, lo], neg_m, p[:, lo], ALU.subtract, ALU.mult, accum_out=gap_lo
        )
        guess_bias = pool.tile([P, 1], F32)
        nc.vector.tensor_scalar(guess_bias[:], neg_m, -1.0, -LN_OFFSET, ALU.mult, ALU.add)
        nc.vector.tensor_tensor(addend[:, c_res : c_res + 1], reserve_sb[:], neg_m, ALU.add)
        nc.vector.scalar_tensor_tensor(p_gain[:, lo], p[:, lo], rescale[:], gain_sb[:, lo], ALU.mult, ALU.mult)
        nc.vector.scalar_tensor_tensor(
            gap_p[:, hi],
            neg_s[:, hi],
            neg_m,
            p[:, hi],
            ALU.subtract,
            ALU.mult,
            accum_out=addend[:, c_den : c_den + 1],
        )

        inv_guess = pool.tile([P, 1], F32)
        nc.scalar.activation(inv_guess[:], z.bitcast(U32), ACT.Exp, scale=-LN_PER_BIT, bias=LN_OFFSET)
        nc.scalar.activation(
            addend[:, c_log : c_log + 1], z.bitcast(U32), ACT.Identity, scale=LN_PER_BIT, bias=guess_bias[:]
        )
        nc.scalar.activation(
            factor[:, 0 : c_log + 1], inv_guess[:].to_broadcast([P, c_log + 1]), ACT.Identity, scale=z, bias=-1.0
        )
        nc.scalar.activation(addend[:, c_one : c_one + 1], gap_lo, ACT.Copy, scale=rescale[:])

        scan = pool.tile([P, steps], F32)
        nc.vector.tensor_tensor_scan(scan[:], factor, addend, 0.0, ALU.mult, ALU.add)
        row_scale = pool.tile([P, 1], F32)
        nc.vector.reciprocal(row_scale[:], scan[:, c_out : c_out + 1])
        nc.vector.tensor_tensor(p_gain[:, hi], p[:, hi], gain_sb[:, hi], ALU.mult)
        neg_log = pool.tile([P, SLOTS], F32)
        nc.vector.tensor_scalar(
            neg_log[:], neg_s[:], scan[:, c_log : c_log + 1], row_scale[:], ALU.add, ALU.mult
        )

        nc.vector.tensor_tensor(placed[:].indirect(list4[:]), p_gain[:], neg_log[:], ALU.mult)

        c0 = 0
        for n, width in enumerate(OUT_WIDTHS):
            cols = slice(c0, c0 + width)
            total = pool.tile([P, width], F32, name=f"total{n}")
            nc.vector.tensor_tensor(total[:], placed[:, cols], old_sb[:, cols], ALU.add)
            queue = nc.sync if n % 2 == 0 else nc.scalar
            queue.dma_start(out=out[:, cols], in_=total[:])
            c0 = c0 + width
